import numpy as np
import ml_dtypes


def mxq(x, axis, fmt="e4m3"):
    dtype, down = {"e4m3": (ml_dtypes.float8_e4m3fn, 7), "e5m2": (ml_dtypes.float8_e5m2, 14)}[fmt]
    v = np.moveaxis(np.asarray(x, np.float32).astype(ml_dtypes.bfloat16).astype(np.float64), axis, -1)
    blocks = v.reshape(v.shape[:-1] + (-1, 32))
    amax = np.abs(blocks).max(-1, keepdims=True)
    byte = np.maximum(np.where(amax > 0, np.frexp(amax)[1] - 1 + 127, 0) - down, 1)
    scale = np.exp2(byte - 127.0)
    codes = (blocks / scale).astype(np.float32).astype(dtype).astype(np.float64)
    return np.moveaxis((codes * scale).reshape(v.shape), -1, axis)


WIDE = False


def mx_kscale(k):
    if not WIDE:
        return np.ones(k)
    levels = np.array([10, -10, 5, -5, 0])
    if k % 512:
        return np.exp2(np.random.permutation(np.resize(levels, k // 32))).repeat(32)
    a = np.empty((k // 512, 16))
    for p in range(k // 512):
        a[p, :8] = np.random.permutation(np.resize(levels, 8))
        for g in range(8):
            far = levels[np.abs(levels - a[p, g]) >= 10]
            a[p, g + 8] = far[np.random.randint(len(far))]
    return np.exp2(a.ravel()).repeat(32)


def f64(x):
    return np.asarray(x).astype(np.float64)


def striped(idx):
    return np.tile(np.asarray(idx).reshape(-1, 16).T, (8, 1)).astype(np.uint16)


def unstriped(offs):
    return offs[:16].T.reshape(-1).astype(np.int64)


E2M1 = np.array([0.0, 0.5, 1.0, 1.5, 2.0, 3.0, 4.0, 6.0, -0.0, -0.5, -1.0, -1.5, -2.0, -3.0, -4.0, -6.0])


def pack_weight(w, fmt):
    k, n = w.shape
    w = f64(np.asarray(w, np.float32).astype(ml_dtypes.bfloat16)).reshape(k // 32, 32, n)
    amax = np.abs(w).max(1)
    if fmt == "e4m3":
        byte = np.frexp(amax)[1] - 1 + 127 - 7
    else:
        mant, ex = np.frexp(amax / 6.0)
        byte = np.where(mant > 0.5, ex, ex - 1) + 127
    byte = np.clip(np.where(amax > 0, byte, 1), 1, 254)
    scaled = (w * np.exp2(127.0 - byte)[:, None, :]).reshape(k, n).astype(np.float32)
    by_word = np.ascontiguousarray(scaled.reshape(k // 512, 128, 4, n).transpose(0, 1, 3, 2))
    if fmt == "e4m3":
        words = by_word.astype(ml_dtypes.float8_e4m3fn).view(np.uint8)
    else:
        c = by_word.astype(ml_dtypes.float4_e2m1fn).view(np.uint8) & 0xF
        words = (c[..., 0::2] | (c[..., 1::2] << 4)).reshape(k // 512, 128, 2 * n)
    return np.ascontiguousarray(words), np.ascontiguousarray(byte.astype(np.uint8).reshape(k // 512, 16, n))


def unpack_weight(words, scales, fmt):
    g, _, n = scales.shape
    words = np.ascontiguousarray(words).reshape(g, 128, n, -1)
    if fmt == "e4m3":
        vals = words.view(ml_dtypes.float8_e4m3fn).astype(np.float64)
    else:
        nib = np.empty((g, 128, n, 4), np.uint8)
        nib[..., 0::2] = words & 0xF
        nib[..., 1::2] = words >> 4
        vals = E2M1[nib]
    vals = vals * np.repeat(np.exp2(scales.astype(np.float64) - 127.0), 8, axis=1)[..., None]
    return vals.transpose(0, 1, 3, 2).reshape(g * 512, n)


def bf(x):
    return np.asarray(x, np.float32).astype(ml_dtypes.bfloat16)


def planes(Y):
    r, m = Y.shape
    b = f64(bf(Y)).reshape(r // 32, 32, m)
    amax = np.abs(b).max(1)
    byte = np.clip(np.where(amax > 0, np.frexp(amax)[1] - 1 + 127 - 7, 1), 1, 254)
    codes = (b * np.exp2(127.0 - byte)[:, None, :]).reshape(r, m).astype(np.float32).astype(ml_dtypes.float8_e4m3fn).view(np.uint8)
    words = codes.reshape(r // 512, 128, 4, m).transpose(0, 1, 3, 2)
    return np.ascontiguousarray(words), np.ascontiguousarray(byte.astype(np.uint8).reshape(r // 512, 16, m))


K, T, J, N, R = 1024, 2048, 512, 512, 512


def setup_inputs():
    n = np.random.standard_normal
    idx = np.random.permutation(T)[:J]
    fk = mx_kscale(K)
    fr = mx_kscale(R)
    xtp = pack_weight(n((K, T)) / fk[:, None], "e2m1")
    wap = pack_weight(n((K, R)) * 1 / np.sqrt(K) * fk[:, None] * fr, "e4m3")
    wbp = pack_weight(n((K, R)) * 1 / np.sqrt(K) * fk[:, None] * fr, "e2m1")
    wdp = pack_weight(n((R, N)) * 1 / np.sqrt(R) / fr[:, None], "e4m3")
    return {
        "xt_words": xtp[0],
        "xt_scales": xtp[1],
        "wa_words": wap[0],
        "wa_scales": wap[1],
        "wb_words": wbp[0],
        "wb_scales": wbp[1],
        "wd_words": wdp[0],
        "wd_scales": wdp[1],
        "ga": (np.random.uniform(0.4, 1.2, (1, J))).astype(np.float32),
        "offs": striped(idx),
    }


def reference(xt_words, xt_scales, wa_words, wa_scales, wb_words, wb_scales, wd_words, wd_scales, ga, offs):
    idx = unstriped(offs)
    xtu = unpack_weight(xt_words, xt_scales, "e2m1")
    wau = unpack_weight(wa_words, wa_scales, "e4m3")
    wbu = unpack_weight(wb_words, wb_scales, "e2m1")
    wdu = unpack_weight(wd_words, wd_scales, "e4m3")
    xtidxg = xtu[:, idx]
    a = wau.T @ xtidxg
    b = wbu.T @ xtidxg
    hid = np.maximum(a - b, 0.0)
    hidq = mxq(hid, 0, "e4m3")
    p = wdu.T @ hidq
    y = p * f64(ga)
    words, scales = planes(y)
    return y, words, scales

@@ -1,0 +1,178 @@
+from contextlib import ExitStack
+
+import concourse.mybir as mybir
+from concourse.masks import make_identity
+
+K, T, J, N, R = 1024, 2048, 512, 512, 512
+FLOPS = 2 * (2 * K * R * J + R * N * J)
+
+F32 = mybir.dt.float32
+BF16 = mybir.dt.bfloat16
+I32 = mybir.dt.int32
+U16 = mybir.dt.uint16
+U8 = mybir.dt.uint8
+FP8X4 = mybir.dt.float8_e4m3fn_x4
+FP4X4 = mybir.dt.float4_e2m1fn_x4
+ALU = mybir.AluOpType
+ACT = mybir.ActivationFunctionType
+
+P = 128
+PACK = 4
+PASSES = K // (P * PACK)
+TILES = J // P
+HALF = J // 2
+
+
+def tile_moe_experts_difference_hidden_pl_kernel(
+    tc, xt_words, xt_scales, wa_words, wa_scales, wb_words, wb_scales, wd_words, wd_scales, ga, offs,
+    out_0, out_1, out_2,
+):
+    nc = tc.nc
+    with ExitStack() as ctx:
+        keep = ctx.enter_context(tc.tile_pool(name="keep", bufs=1))
+        ring = ctx.enter_context(tc.tile_pool(name="ring", bufs=2))
+        psum = ctx.enter_context(tc.psum_pool(name="psum", bufs=2))
+
+        offsets = keep.tile([P, J // 16], U16, name="offsets")
+        xs_win = keep.tile([P, T], U8, name="xs_win", tag="early_late", align_bytes=64)
+        xw_win = [keep.tile([P, T], U16, name=f"xw_win{z}", align_bytes=64) for z in range(PASSES)]
+        wa_w = keep.tile([P, PASSES, R], I32, name="wa_w", align_bytes=64)
+        wb_w = keep.tile([P, PASSES, R], U16, name="wb_w", align_bytes=64)
+        wa_s = keep.tile([P, PASSES, R], U8, name="wa_s", align_bytes=64)
+        wb_s = keep.tile([P, PASSES, R], U8, name="wb_s", align_bytes=64)
+        wd_s = keep.tile([P, N], U8, name="wd_s", align_bytes=64)
+        x_s = keep.tile([P, PASSES, J], U8, name="x_s", align_bytes=64)
+        xs_got = keep.tile([P, J], U8, name="xs_got", align_bytes=64)
+        ga_col = keep.tile([P, TILES], F32, name="ga_col")
+        ga_all = keep.tile([P, J], F32, name="ga_all")
+        ident = keep.tile([P, P], F32, name="ident")
+
+        def flat_i32(t):
+            return t[:].rearrange("p z n -> p (z n)").bitcast(I32)
+
+        def load_scale_rows(eng, plane, rows):
+            by_row = rows.rearrange("z q n -> q z n").bitcast(I32)
+            for r in range(4):
+                eng.dma_start(out=plane[r:P:32].bitcast(I32), in_=by_row[r:16:4])
+
+        nc.sync.dma_start(offsets[:], offs)
+        nc.scalar.dma_start(
+            out=xs_win[0:32, :].bitcast(I32), in_=xt_scales.rearrange("z q n -> q z n").bitcast(I32)
+        )
+        nc.vector.memset(flat_i32(wb_s), 0)
+        nc.vector.memset(xs_win[32:64, :].bitcast(I32), 0)
+        nc.vector.memset(xs_win[64:P, :].bitcast(I32), 0)
+        nc.vector.memset(flat_i32(x_s), 0)
+        nc.vector.memset(wd_s[:].bitcast(I32), 0)
+        make_identity(nc, ident[:])
+        nc.gpsimd.memset(flat_i32(wa_s), 0)
+
+        load_scale_rows(nc.scalar, wb_s, wb_scales)
+        nc.gpsimd.dma_start(out=ga_col[:], in_=ga.rearrange("o (p i) -> (o p) i", i=TILES))
+        load_scale_rows(nc.gpsimd, wa_s, wa_scales)
+        for z in range(PASSES):
+            nc.sync.dma_start(out=xw_win[z][:].bitcast(I32), in_=xt_words[z].bitcast(I32))
+        nc.sync.dma_start(out=wb_w[:].bitcast(I32), in_=wb_words.rearrange("z p n -> p z n").bitcast(I32))
+        nc.sync.dma_start(out=wa_w[:], in_=wa_words.rearrange("z p n t -> p z (n t)").bitcast(I32))
+        for r in range(4):
+            nc.sync.dma_start(out=wd_s[r:P:32, :].bitcast(I32), in_=wd_scales[0].bitcast(I32)[r:16:4])
+
+        ga_ps = psum.tile([P, TILES, P], F32, name="ga_ps", tag="p")
+        for i in range(TILES):
+            nc.tensor.transpose(ga_ps[:, i, :], ga_col[:, i : i + 1].to_broadcast([P, P]), ident[:])
+        nc.scalar.copy(out=ga_all[:].rearrange("q (p i) -> q p i", i=TILES), in_=ga_ps[:].rearrange("q i p -> q p i"))
+
+        nc.vector.tensor_copy(xs_got[:], xs_win[:].indirect(offsets[:]))
+        for q in range(4):
+            nc.scalar.dma_start(
+                out=x_s[32 * q : 32 * q + 4].bitcast(I32), in_=xs_got[8 * q : 8 * q + 8, :].bitcast(I32)
+            )
+        x_w = {}
+        for h in range(2):
+            for z in range(PASSES):
+                x_w[z, h] = keep.tile([P, HALF], U16, name=f"x_w{z}{h}", align_bytes=64)
+                nc.vector.tensor_copy(x_w[z, h][:], xw_win[z][:].indirect(offsets[:, 16 * h : 16 * h + 16]))
+
+        wd_w = keep.tile([P, N], I32, name="wd_w", tag="early_late", align_bytes=64)
+        nc.sync.dma_start(out=wd_w[:], in_=wd_words[0].rearrange("p n t -> p (n t)").bitcast(I32))
+        wdp_w = keep.tile([P, PACK, P], I32, name="wdp_w", align_bytes=64)
+        wdp_s = keep.tile([P, PACK, P], U8, name="wdp_s", align_bytes=64)
+        nc.vector.tensor_copy(
+            out=wdp_w[:].rearrange("p t (c i) -> p c t i", i=4), in_=wd_w[:].rearrange("p (c i t) -> p c t i", i=4, t=PACK)
+        )
+        nc.vector.tensor_copy(
+            out=wdp_s[:].rearrange("p t (c i) -> p c t i", i=16), in_=wd_s[:].rearrange("p (c i t) -> p c t i", i=16, t=PACK)
+        )
+
+        y_w = keep.tile([P, J], I32, name="y_w", align_bytes=64)
+        y_s = keep.tile([P, J], U8, name="y_s", align_bytes=64)
+        out_rows = out_0.rearrange("(p t) j -> p t j", t=PACK)
+        out_words = out_1[0].rearrange("p c t -> p (c t)").bitcast(I32)
+        gap, hid_w, hid_s = {}, {}, {}
+
+        def experts(i):
+            tok = slice(P * i, P * (i + 1))
+            h, lo = divmod(P * i, HALF)
+            b_ps = psum.tile([P, R], F32, name="b_ps", tag="b")
+            a_ps = psum.tile([P, R], F32, name="a_ps", tag="a")
+            for acc, w, s, fmt in ((b_ps, wb_w, wb_s, FP4X4), (a_ps, wa_w, wa_s, FP8X4)):
+                for z in range(PASSES):
+                    nc.tensor.matmul_mx(
+                        out=acc[:], lhsT=x_w[z, h][:, lo : lo + P].bitcast(FP4X4), lhsT_scale=x_s[:, z, tok],
+                        rhs=w[:, z, :].bitcast(fmt), rhs_scale=s[:, z, :], start=(z == 0), stop=(z == PASSES - 1),
+                    )
+            b_sb = ring.tile([P, 2, P, 2], F32, name="b_sb")
+            nc.scalar.copy(out=b_sb[:], in_=b_ps[:].rearrange("j (p u e) -> j u p e", u=2, e=2))
+            gap[i] = ring.tile([P, 2, P, 2], BF16, name="gap", align_bytes=64)
+            nc.vector.tensor_tensor(
+                out=gap[i][:], in0=a_ps[:].rearrange("j (p u e) -> j u p e", u=2, e=2), in1=b_sb[:], op=ALU.subtract
+            )
+
+        def turn(i):
+            pairs = gap[i][:].rearrange("j u p e -> j (u p e)").bitcast(F32)
+            tr_ps = psum.tile([P, 2 * P], F32, name="tr_ps", tag="tr")
+            for u in range(2):
+                nc.tensor.transpose(tr_ps[:, P * u : P * (u + 1)], pairs[:, P * u : P * (u + 1)], ident[:])
+            hid = ring.tile([P, P, 2, 2], BF16, name="hid", align_bytes=64)
+            nc.scalar.activation(
+                out=hid[:], in_=tr_ps[:].bitcast(BF16).rearrange("p (u j e) -> p j u e", u=2, e=2), func=ACT.Relu
+            )
+            hid_w[i] = ring.tile([P, P], I32, name="hid_w", align_bytes=64)
+            hid_s[i] = ring.tile([P, P], U8, name="hid_s", align_bytes=64)
+            nc.vector.quantize_mx(
+                out=hid_w[i][:].bitcast(FP8X4), scales=hid_s[i][:], in_=hid[:].rearrange("p j u e -> p (j u e)")
+            )
+
+        def shared(i):
+            tok = slice(P * i, P * (i + 1))
+            p_ps = psum.tile([P, PACK, P], F32, name="p_ps", tag="p")
+            for t in range(PACK):
+                nc.tensor.matmul_mx(
+                    out=p_ps[:, t, :], lhsT=wdp_w[:, t, :].bitcast(FP8X4), lhsT_scale=wdp_s[:, t, :],
+                    rhs=hid_w[i][:].bitcast(FP8X4), rhs_scale=hid_s[i][:], start=True, stop=True,
+                )
+            y = keep.tile([P, PACK, P], F32, name=f"y{i}")
+            nc.vector.tensor_tensor(
+                out=y[:], in0=p_ps[:], in1=ga_all[:, tok].unsqueeze(1).to_broadcast([P, PACK, P]), op=ALU.mult
+            )
+            nc.sync.dma_start(out=out_rows[:, :, tok], in_=y[:])
+            y16 = ring.tile([P, P, PACK], BF16, name="y16", align_bytes=64)
+            nc.scalar.copy(
+                out=y16[:].rearrange("p (c i) t -> p c t i", i=4), in_=y[:].rearrange("p t (c i) -> p c t i", i=4)
+            )
+            nc.vector.quantize_mx(
+                out=y_w[:, tok].bitcast(FP8X4), scales=y_s[:, tok], in_=y16[:].rearrange("p j t -> p (j t)")
+            )
+            nc.sync.dma_start(out=out_words[:, tok], in_=y_w[:, tok])
+
+        for step in range(TILES + 2):
+            if step < TILES:
+                experts(step)
+            if 1 <= step <= TILES:
+                turn(step - 1)
+            if step >= 2:
+                shared(step - 2)
+
+        for q in range(4):
+            eng = nc.sync if q % 2 == 0 else nc.scalar
+            eng.dma_start(out=out_2[0].bitcast(I32)[4 * q : 4 * q + 4], in_=y_s[32 * q : 32 * q + 4, :].bitcast(I32))

@@ -21,6 +21,7 @@ PACK = 4
 PASSES = K // (P * PACK)
 TILES = J // P
 HALF = J // 2
+WARM = 4
 
 
 def tile_moe_experts_difference_hidden_pl_kernel(
@@ -30,8 +31,8 @@ def tile_moe_experts_difference_hidden_pl_kernel(
     nc = tc.nc
     with ExitStack() as ctx:
         keep = ctx.enter_context(tc.tile_pool(name="keep", bufs=1))
-        ring = ctx.enter_context(tc.tile_pool(name="ring", bufs=2))
-        psum = ctx.enter_context(tc.psum_pool(name="psum", bufs=2))
+        ring = ctx.enter_context(tc.tile_pool(name="ring", bufs=TILES))
+        psum = ctx.enter_context(tc.psum_pool(name="psum", bufs=1))
 
         offsets = keep.tile([P, J // 16], U16, name="offsets")
         xs_win = keep.tile([P, T], U8, name="xs_win", tag="early_late", align_bytes=64)
@@ -40,9 +41,9 @@ def tile_moe_experts_difference_hidden_pl_kernel(
         wb_w = keep.tile([P, PASSES, R], U16, name="wb_w", align_bytes=64)
         wa_s = keep.tile([P, PASSES, R], U8, name="wa_s", align_bytes=64)
         wb_s = keep.tile([P, PASSES, R], U8, name="wb_s", align_bytes=64)
-        wd_s = keep.tile([P, N], U8, name="wd_s", align_bytes=64)
         x_s = keep.tile([P, PASSES, J], U8, name="x_s", align_bytes=64)
         xs_got = keep.tile([P, J], U8, name="xs_got", align_bytes=64)
+        wd_s = keep.tile([P, N], U8, name="wd_s", align_bytes=64)
         ga_col = keep.tile([P, TILES], F32, name="ga_col")
         ga_all = keep.tile([P, J], F32, name="ga_all")
         ident = keep.tile([P, P], F32, name="ident")
@@ -63,24 +64,19 @@ def tile_moe_experts_difference_hidden_pl_kernel(
         nc.vector.memset(xs_win[32:64, :].bitcast(I32), 0)
         nc.vector.memset(xs_win[64:P, :].bitcast(I32), 0)
         nc.vector.memset(flat_i32(x_s), 0)
-        nc.vector.memset(wd_s[:].bitcast(I32), 0)
+        nc.vector.memset(flat_i32(wa_s), 0)
+        nc.gpsimd.memset(wd_s[:].bitcast(I32), 0)
         make_identity(nc, ident[:])
-        nc.gpsimd.memset(flat_i32(wa_s), 0)
+        nc.gpsimd.dma_start(out=ga_col[:], in_=ga.rearrange("o (p i) -> (o p) i", i=TILES))
+        for r in range(4):
+            nc.gpsimd.dma_start(out=wd_s[r:P:32, :].bitcast(I32), in_=wd_scales[0].bitcast(I32)[r:16:4])
 
         load_scale_rows(nc.scalar, wb_s, wb_scales)
-        nc.gpsimd.dma_start(out=ga_col[:], in_=ga.rearrange("o (p i) -> (o p) i", i=TILES))
-        load_scale_rows(nc.gpsimd, wa_s, wa_scales)
+        nc.sync.dma_start(out=wb_w[:].bitcast(I32), in_=wb_words.rearrange("z p n -> p z n").bitcast(I32))
         for z in range(PASSES):
             nc.sync.dma_start(out=xw_win[z][:].bitcast(I32), in_=xt_words[z].bitcast(I32))
-        nc.sync.dma_start(out=wb_w[:].bitcast(I32), in_=wb_words.rearrange("z p n -> p z n").bitcast(I32))
         nc.sync.dma_start(out=wa_w[:], in_=wa_words.rearrange("z p n t -> p z (n t)").bitcast(I32))
-        for r in range(4):
-            nc.sync.dma_start(out=wd_s[r:P:32, :].bitcast(I32), in_=wd_scales[0].bitcast(I32)[r:16:4])
-
-        ga_ps = psum.tile([P, TILES, P], F32, name="ga_ps", tag="p")
-        for i in range(TILES):
-            nc.tensor.transpose(ga_ps[:, i, :], ga_col[:, i : i + 1].to_broadcast([P, P]), ident[:])
-        nc.scalar.copy(out=ga_all[:].rearrange("q (p i) -> q p i", i=TILES), in_=ga_ps[:].rearrange("q i p -> q p i"))
+        load_scale_rows(nc.sync, wa_s, wa_scales)
 
         nc.vector.tensor_copy(xs_got[:], xs_win[:].indirect(offsets[:]))
         for q in range(4):
@@ -110,27 +106,41 @@ def tile_moe_experts_difference_hidden_pl_kernel(
         out_words = out_1[0].rearrange("p c t -> p (c t)").bitcast(I32)
         gap, hid_w, hid_s = {}, {}, {}
 
-        def experts(i):
-            tok = slice(P * i, P * (i + 1))
+        b_sb = {}
+
+        def product(i, acc, w, s, fmt):
             h, lo = divmod(P * i, HALF)
-            b_ps = psum.tile([P, R], F32, name="b_ps", tag="b")
-            a_ps = psum.tile([P, R], F32, name="a_ps", tag="a")
-            for acc, w, s, fmt in ((b_ps, wb_w, wb_s, FP4X4), (a_ps, wa_w, wa_s, FP8X4)):
-                for z in range(PASSES):
-                    nc.tensor.matmul_mx(
-                        out=acc[:], lhsT=x_w[z, h][:, lo : lo + P].bitcast(FP4X4), lhsT_scale=x_s[:, z, tok],
-                        rhs=w[:, z, :].bitcast(fmt), rhs_scale=s[:, z, :], start=(z == 0), stop=(z == PASSES - 1),
-                    )
-            b_sb = ring.tile([P, 2, P, 2], F32, name="b_sb")
-            nc.scalar.copy(out=b_sb[:], in_=b_ps[:].rearrange("j (p u e) -> j u p e", u=2, e=2))
+            for z in range(PASSES):
+                nc.tensor.matmul_mx(
+                    out=acc[:], lhsT=x_w[z, h][:, lo : lo + P].bitcast(FP4X4), lhsT_scale=x_s[:, z, P * i : P * (i + 1)],
+                    rhs=w[:, z, :].bitcast(fmt), rhs_scale=s[:, z, :], start=(z == 0), stop=(z == PASSES - 1),
+                )
+
+        def second(i):
+            b_ps = psum.tile([P, R], F32, name="b_ps", tag=f"b{i}")
+            product(i, b_ps, wb_w, wb_s, FP4X4)
+            b_sb[i] = keep.tile([P, 2, P, 2], F32, name=f"b_sb{i}")
+            nc.scalar.copy(out=b_sb[i][:], in_=b_ps[:].rearrange("j (p u e) -> j u p e", u=2, e=2))
+
+        def first(i):
+            a_ps = psum.tile([P, R], F32, name="a_ps", tag=f"a{i}")
+            product(i, a_ps, wa_w, wa_s, FP8X4)
             gap[i] = ring.tile([P, 2, P, 2], BF16, name="gap", align_bytes=64)
             nc.vector.tensor_tensor(
-                out=gap[i][:], in0=a_ps[:].rearrange("j (p u e) -> j u p e", u=2, e=2), in1=b_sb[:], op=ALU.subtract
+                out=gap[i][:], in0=a_ps[:].rearrange("j (p u e) -> j u p e", u=2, e=2), in1=b_sb[i][:], op=ALU.subtract
+            )
+
+        def spread_gate():
+            ga_ps = psum.tile([P, TILES, P], F32, name="ga_ps", tag="b3")
+            for i in range(TILES):
+                nc.tensor.transpose(ga_ps[:, i, :], ga_col[:, i : i + 1].to_broadcast([P, P]), ident[:])
+            nc.vector.tensor_copy(
+                out=ga_all[:].rearrange("q (p i) -> q p i", i=TILES), in_=ga_ps[:].rearrange("q i p -> q p i")
             )
 
         def turn(i):
             pairs = gap[i][:].rearrange("j u p e -> j (u p e)").bitcast(F32)
-            tr_ps = psum.tile([P, 2 * P], F32, name="tr_ps", tag="tr")
+            tr_ps = psum.tile([P, 2 * P], F32, name="tr_ps", tag=f"a{i}")
             for u in range(2):
                 nc.tensor.transpose(tr_ps[:, P * u : P * (u + 1)], pairs[:, P * u : P * (u + 1)], ident[:])
             hid = ring.tile([P, P, 2, 2], BF16, name="hid", align_bytes=64)
@@ -145,33 +155,55 @@ def tile_moe_experts_difference_hidden_pl_kernel(
 
         def shared(i):
             tok = slice(P * i, P * (i + 1))
-            p_ps = psum.tile([P, PACK, P], F32, name="p_ps", tag="p")
+            p_ps = psum.tile([P, PACK, P], F32, name="p_ps", tag=f"a{i}")
             for t in range(PACK):
                 nc.tensor.matmul_mx(
                     out=p_ps[:, t, :], lhsT=wdp_w[:, t, :].bitcast(FP8X4), lhsT_scale=wdp_s[:, t, :],
                     rhs=hid_w[i][:].bitcast(FP8X4), rhs_scale=hid_s[i][:], start=True, stop=True,
                 )
             y = keep.tile([P, PACK, P], F32, name=f"y{i}")
+            y16 = ring.tile([P, P, PACK], BF16, name="y16", align_bytes=64)
+            if i == TILES - 1:
+                nc.vector.tensor_tensor(
+                    out=y16[:], in0=p_ps[:].rearrange("p t j -> p j t"),
+                    in1=ga_all[:, tok].unsqueeze(2).to_broadcast([P, P, PACK]), op=ALU.mult,
+                )
             nc.vector.tensor_tensor(
                 out=y[:], in0=p_ps[:], in1=ga_all[:, tok].unsqueeze(1).to_broadcast([P, PACK, P]), op=ALU.mult
             )
             nc.sync.dma_start(out=out_rows[:, :, tok], in_=y[:])
-            y16 = ring.tile([P, P, PACK], BF16, name="y16", align_bytes=64)
-            nc.scalar.copy(
-                out=y16[:].rearrange("p (c i) t -> p c t i", i=4), in_=y[:].rearrange("p t (c i) -> p c t i", i=4)
-            )
+            if i < TILES - 1:
+                nc.scalar.copy(
+                    out=y16[:].rearrange("p (c i) t -> p c t i", i=4), in_=y[:].rearrange("p t (c i) -> p c t i", i=4)
+                )
             nc.vector.quantize_mx(
                 out=y_w[:, tok].bitcast(FP8X4), scales=y_s[:, tok], in_=y16[:].rearrange("p j t -> p (j t)")
             )
             nc.sync.dma_start(out=out_words[:, tok], in_=y_w[:, tok])
 
-        for step in range(TILES + 2):
-            if step < TILES:
-                experts(step)
-            if 1 <= step <= TILES:
-                turn(step - 1)
-            if step >= 2:
-                shared(step - 2)
+        warm = psum.tile([P, R], F32, name="warm", tag="a3")
+        for k in range(WARM):
+            nc.tensor.matmul_mx(
+                out=warm[:], lhsT=wb_w[:, 0, 0:P].bitcast(FP4X4), lhsT_scale=wb_s[:, 0, 0:P],
+                rhs=wb_w[:, 0, :].bitcast(FP4X4), rhs_scale=wb_s[:, 0, :], start=True, stop=True,
+            )
+        spread_gate()
+        second(0)
+        second(1)
+        first(0)
+        second(2)
+        first(1)
+        turn(0)
+        second(3)
+        first(2)
+        turn(1)
+        first(3)
+        shared(0)
+        turn(2)
+        turn(3)
+        shared(1)
+        shared(2)
+        shared(3)
 
         for q in range(4):
             eng = nc.sync if q % 2 == 0 else nc.scalar

@@ -22,6 +22,7 @@ PASSES = K // (P * PACK)
 TILES = J // P
 HALF = J // 2
 WARM = 4
+ROW0 = 96
 
 
 def tile_moe_experts_difference_hidden_pl_kernel(
@@ -35,14 +36,14 @@ def tile_moe_experts_difference_hidden_pl_kernel(
         psum = ctx.enter_context(tc.psum_pool(name="psum", bufs=1))
 
         offsets = keep.tile([P, J // 16], U16, name="offsets")
-        xs_win = keep.tile([P, T], U8, name="xs_win", tag="early_late", align_bytes=64)
+        xs_win = keep.tile([P, T], U8, name="xs_win", align_bytes=64)
         xw_win = [keep.tile([P, T], U16, name=f"xw_win{z}", align_bytes=64) for z in range(PASSES)]
         wa_w = keep.tile([P, PASSES, R], I32, name="wa_w", align_bytes=64)
         wb_w = keep.tile([P, PASSES, R], U16, name="wb_w", align_bytes=64)
         wa_s = keep.tile([P, PASSES, R], U8, name="wa_s", align_bytes=64)
         wb_s = keep.tile([P, PASSES, R], U8, name="wb_s", align_bytes=64)
         x_s = keep.tile([P, PASSES, J], U8, name="x_s", align_bytes=64)
-        xs_got = keep.tile([P, J], U8, name="xs_got", align_bytes=64)
+        xs_got = keep.tile([P, J], U8, name="xs_got", tag="early_late", align_bytes=64)
         wd_s = keep.tile([P, N], U8, name="wd_s", align_bytes=64)
         ga_col = keep.tile([P, TILES], F32, name="ga_col")
         ga_all = keep.tile([P, J], F32, name="ga_all")
@@ -58,11 +59,12 @@ def tile_moe_experts_difference_hidden_pl_kernel(
 
         nc.sync.dma_start(offsets[:], offs)
         nc.scalar.dma_start(
-            out=xs_win[0:32, :].bitcast(I32), in_=xt_scales.rearrange("z q n -> q z n").bitcast(I32)
+            out=xs_win[ROW0:P, :].bitcast(I32), in_=xt_scales.rearrange("z q n -> q z n").bitcast(I32)
         )
         nc.vector.memset(flat_i32(wb_s), 0)
-        nc.vector.memset(xs_win[32:64, :].bitcast(I32), 0)
-        nc.vector.memset(xs_win[64:P, :].bitcast(I32), 0)
+        nc.vector.memset(xs_win[0:ROW0, :].bitcast(I32), 0)
+        table_in = keep.tile([P, 1], F32, name="table_in")
+        nc.vector.memset(table_in[:], 0.0)
         nc.vector.memset(flat_i32(x_s), 0)
         nc.vector.memset(flat_i32(wa_s), 0)
         nc.gpsimd.memset(wd_s[:].bitcast(I32), 0)
@@ -72,6 +74,8 @@ def tile_moe_experts_difference_hidden_pl_kernel(
             nc.gpsimd.dma_start(out=wd_s[r:P:32, :].bitcast(I32), in_=wd_scales[0].bitcast(I32)[r:16:4])
 
         load_scale_rows(nc.scalar, wb_s, wb_scales)
+        table_out = keep.tile([P, 1], F32, name="table_out")
+        nc.scalar.activation(out=table_out[:], in_=table_in[:], func=ACT.Relu)
         nc.sync.dma_start(out=wb_w[:].bitcast(I32), in_=wb_words.rearrange("z p n -> p z n").bitcast(I32))
         for z in range(PASSES):
             nc.sync.dma_start(out=xw_win[z][:].bitcast(I32), in_=xt_words[z].bitcast(I32))
@@ -81,7 +85,7 @@ def tile_moe_experts_difference_hidden_pl_kernel(
         nc.vector.tensor_copy(xs_got[:], xs_win[:].indirect(offsets[:]))
         for q in range(4):
             nc.scalar.dma_start(
-                out=x_s[32 * q : 32 * q + 4].bitcast(I32), in_=xs_got[8 * q : 8 * q + 8, :].bitcast(I32)
+                out=x_s[32 * q : 32 * q + 4].bitcast(I32), in_=xs_got[ROW0 + 8 * q : ROW0 + 8 * q + 8, :].bitcast(I32)
             )
         x_w = {}
         for h in range(2):
@@ -91,14 +95,6 @@ def tile_moe_experts_difference_hidden_pl_kernel(
 
         wd_w = keep.tile([P, N], I32, name="wd_w", tag="early_late", align_bytes=64)
         nc.sync.dma_start(out=wd_w[:], in_=wd_words[0].rearrange("p n t -> p (n t)").bitcast(I32))
-        wdp_w = keep.tile([P, PACK, P], I32, name="wdp_w", align_bytes=64)
-        wdp_s = keep.tile([P, PACK, P], U8, name="wdp_s", align_bytes=64)
-        nc.vector.tensor_copy(
-            out=wdp_w[:].rearrange("p t (c i) -> p c t i", i=4), in_=wd_w[:].rearrange("p (c i t) -> p c t i", i=4, t=PACK)
-        )
-        nc.vector.tensor_copy(
-            out=wdp_s[:].rearrange("p t (c i) -> p c t i", i=16), in_=wd_s[:].rearrange("p (c i t) -> p c t i", i=16, t=PACK)
-        )
 
         y_w = keep.tile([P, J], I32, name="y_w", align_bytes=64)
         y_s = keep.tile([P, J], U8, name="y_s", align_bytes=64)
@@ -119,7 +115,7 @@ def tile_moe_experts_difference_hidden_pl_kernel(
         def second(i):
             b_ps = psum.tile([P, R], F32, name="b_ps", tag=f"b{i}")
             product(i, b_ps, wb_w, wb_s, FP4X4)
-            b_sb[i] = keep.tile([P, 2, P, 2], F32, name=f"b_sb{i}")
+            b_sb[i] = keep.tile([P, 2, P, 2], F32, name=f"b_sb{i}", tag=f"b_sb{i}", align_bytes=64)
             nc.scalar.copy(out=b_sb[i][:], in_=b_ps[:].rearrange("j (p u e) -> j u p e", u=2, e=2))
 
         def first(i):
@@ -131,10 +127,10 @@ def tile_moe_experts_difference_hidden_pl_kernel(
             )
 
         def spread_gate():
-            ga_ps = psum.tile([P, TILES, P], F32, name="ga_ps", tag="b3")
+            ga_ps = psum.tile([P, TILES, P], F32, name="ga_ps", tag="b0")
             for i in range(TILES):
                 nc.tensor.transpose(ga_ps[:, i, :], ga_col[:, i : i + 1].to_broadcast([P, P]), ident[:])
-            nc.vector.tensor_copy(
+            nc.scalar.copy(
                 out=ga_all[:].rearrange("q (p i) -> q p i", i=TILES), in_=ga_ps[:].rearrange("q i p -> q p i")
             )
 
@@ -187,13 +183,21 @@ def tile_moe_experts_difference_hidden_pl_kernel(
                 out=warm[:], lhsT=wb_w[:, 0, 0:P].bitcast(FP4X4), lhsT_scale=wb_s[:, 0, 0:P],
                 rhs=wb_w[:, 0, :].bitcast(FP4X4), rhs_scale=wb_s[:, 0, :], start=True, stop=True,
             )
-        spread_gate()
         second(0)
         second(1)
-        first(0)
         second(2)
+        first(0)
+        wdp_w = keep.tile([P, PACK, P], I32, name="wdp_w", tag="b_sb0", align_bytes=64)
+        nc.vector.tensor_copy(
+            out=wdp_w[:].rearrange("p t (c i) -> p c t i", i=4), in_=wd_w[:].rearrange("p (c i t) -> p c t i", i=4, t=PACK)
+        )
         first(1)
+        wdp_s = keep.tile([P, PACK, P], U8, name="wdp_s", tag="b_sb1", align_bytes=64)
+        nc.vector.tensor_copy(
+            out=wdp_s[:].rearrange("p t (c i) -> p c t i", i=16), in_=wd_s[:].rearrange("p (c i t) -> p c t i", i=16, t=PACK)
+        )
         turn(0)
+        spread_gate()
         second(3)
         first(2)
         turn(1)

@@ -19,10 +19,16 @@ ACT = mybir.ActivationFunctionType
 P = 128
 PACK = 4
 PASSES = K // (P * PACK)
+QUAD = 32
+QUADS = P // QUAD
+LIVE = 4
+BLOCKS = QUADS * LIVE
 TILES = J // P
 HALF = J // 2
-WARM = 4
-ROW0 = 96
+LIST_ROWS = 16
+SCALE_ROW0 = P - PASSES * BLOCKS
+LINE_WORDS, LINE_BYTES = 4, 16
+WARM_PASSES = 4
 
 
 def tile_moe_experts_difference_hidden_pl_kernel(
@@ -35,74 +41,77 @@ def tile_moe_experts_difference_hidden_pl_kernel(
         ring = ctx.enter_context(tc.tile_pool(name="ring", bufs=TILES))
         psum = ctx.enter_context(tc.psum_pool(name="psum", bufs=1))
 
-        offsets = keep.tile([P, J // 16], U16, name="offsets")
-        xs_win = keep.tile([P, T], U8, name="xs_win", align_bytes=64)
+        offsets = keep.tile([P, J // LIST_ROWS], U16, name="offsets")
+        xs_win = keep.tile([P, T], U8, name="xs_win", tag="window", align_bytes=64)
         xw_win = [keep.tile([P, T], U16, name=f"xw_win{z}", align_bytes=64) for z in range(PASSES)]
         wa_w = keep.tile([P, PASSES, R], I32, name="wa_w", align_bytes=64)
         wb_w = keep.tile([P, PASSES, R], U16, name="wb_w", align_bytes=64)
         wa_s = keep.tile([P, PASSES, R], U8, name="wa_s", align_bytes=64)
         wb_s = keep.tile([P, PASSES, R], U8, name="wb_s", align_bytes=64)
         x_s = keep.tile([P, PASSES, J], U8, name="x_s", align_bytes=64)
-        xs_got = keep.tile([P, J], U8, name="xs_got", tag="early_late", align_bytes=64)
+        xs_got = keep.tile([P, J], U8, name="xs_got", tag="gathered_scales", align_bytes=64)
         wd_s = keep.tile([P, N], U8, name="wd_s", align_bytes=64)
         ga_col = keep.tile([P, TILES], F32, name="ga_col")
         ga_all = keep.tile([P, J], F32, name="ga_all")
         ident = keep.tile([P, P], F32, name="ident")
 
-        def flat_i32(t):
-            return t[:].rearrange("p z n -> p (z n)").bitcast(I32)
+        def flat_i32(planes):
+            return planes[:].rearrange("p z n -> p (z n)").bitcast(I32)
 
-        def load_scale_rows(eng, plane, rows):
+        def load_planes(engine, planes, rows):
             by_row = rows.rearrange("z q n -> q z n").bitcast(I32)
-            for r in range(4):
-                eng.dma_start(out=plane[r:P:32].bitcast(I32), in_=by_row[r:16:4])
+            for r in range(LIVE):
+                engine.dma_start(out=planes[r:P:QUAD].bitcast(I32), in_=by_row[r:BLOCKS:LIVE])
 
         nc.sync.dma_start(offsets[:], offs)
         nc.scalar.dma_start(
-            out=xs_win[ROW0:P, :].bitcast(I32), in_=xt_scales.rearrange("z q n -> q z n").bitcast(I32)
+            out=xs_win[SCALE_ROW0:P, :].bitcast(I32), in_=xt_scales.rearrange("z q n -> q z n").bitcast(I32)
         )
         nc.vector.memset(flat_i32(wb_s), 0)
-        nc.vector.memset(xs_win[0:ROW0, :].bitcast(I32), 0)
-        table_in = keep.tile([P, 1], F32, name="table_in")
-        nc.vector.memset(table_in[:], 0.0)
-        nc.vector.memset(flat_i32(x_s), 0)
+        nc.vector.memset(xs_win[0:SCALE_ROW0, :].bitcast(I32), 0)
         nc.vector.memset(flat_i32(wa_s), 0)
-        nc.gpsimd.memset(wd_s[:].bitcast(I32), 0)
+        nc.vector.memset(flat_i32(x_s), 0)
         make_identity(nc, ident[:])
+        nc.gpsimd.memset(wd_s[:].bitcast(I32), 0)
+        nc.gpsimd.dma_start(out=wa_w[:], in_=wa_words.rearrange("z p n t -> p z (n t)").bitcast(I32))
         nc.gpsimd.dma_start(out=ga_col[:], in_=ga.rearrange("o (p i) -> (o p) i", i=TILES))
-        for r in range(4):
-            nc.gpsimd.dma_start(out=wd_s[r:P:32, :].bitcast(I32), in_=wd_scales[0].bitcast(I32)[r:16:4])
 
-        load_scale_rows(nc.scalar, wb_s, wb_scales)
-        table_out = keep.tile([P, 1], F32, name="table_out")
-        nc.scalar.activation(out=table_out[:], in_=table_in[:], func=ACT.Relu)
+        load_planes(nc.scalar, wb_s, wb_scales)
         nc.sync.dma_start(out=wb_w[:].bitcast(I32), in_=wb_words.rearrange("z p n -> p z n").bitcast(I32))
         for z in range(PASSES):
             nc.sync.dma_start(out=xw_win[z][:].bitcast(I32), in_=xt_words[z].bitcast(I32))
-        nc.sync.dma_start(out=wa_w[:], in_=wa_words.rearrange("z p n t -> p z (n t)").bitcast(I32))
-        load_scale_rows(nc.sync, wa_s, wa_scales)
+        load_planes(nc.sync, wa_s, wa_scales)
+        for r in range(LIVE):
+            nc.sync.dma_start(out=wd_s[r:P:QUAD, :].bitcast(I32), in_=wd_scales[0].bitcast(I32)[r:BLOCKS:LIVE])
 
         nc.vector.tensor_copy(xs_got[:], xs_win[:].indirect(offsets[:]))
-        for q in range(4):
+        for q in range(QUADS):
+            src = SCALE_ROW0 + PASSES * LIVE * q
             nc.scalar.dma_start(
-                out=x_s[32 * q : 32 * q + 4].bitcast(I32), in_=xs_got[ROW0 + 8 * q : ROW0 + 8 * q + 8, :].bitcast(I32)
+                out=x_s[QUAD * q : QUAD * q + LIVE].bitcast(I32), in_=xs_got[src : src + PASSES * LIVE, :].bitcast(I32)
             )
+        table_in = keep.tile([P, 1], F32, name="table_in", tag="window", align_bytes=64)
+        nc.vector.memset(table_in[:], 0.0)
+        table_out = keep.tile([P, 1], F32, name="table_out")
+        nc.scalar.activation(out=table_out[:], in_=table_in[:], func=ACT.Relu)
         x_w = {}
-        for h in range(2):
+        for h in range(J // HALF):
             for z in range(PASSES):
+                picks = offsets[:, h * HALF // LIST_ROWS : (h + 1) * HALF // LIST_ROWS]
                 x_w[z, h] = keep.tile([P, HALF], U16, name=f"x_w{z}{h}", align_bytes=64)
-                nc.vector.tensor_copy(x_w[z, h][:], xw_win[z][:].indirect(offsets[:, 16 * h : 16 * h + 16]))
+                nc.vector.tensor_copy(x_w[z, h][:], xw_win[z][:].indirect(picks))
 
-        wd_w = keep.tile([P, N], I32, name="wd_w", tag="early_late", align_bytes=64)
+        wd_w = keep.tile([P, N], I32, name="wd_w", tag="gathered_scales", align_bytes=64)
         nc.sync.dma_start(out=wd_w[:], in_=wd_words[0].rearrange("p n t -> p (n t)").bitcast(I32))
 
         y_w = keep.tile([P, J], I32, name="y_w", align_bytes=64)
         y_s = keep.tile([P, J], U8, name="y_s", align_bytes=64)
         out_rows = out_0.rearrange("(p t) j -> p t j", t=PACK)
         out_words = out_1[0].rearrange("p c t -> p (c t)").bitcast(I32)
-        gap, hid_w, hid_s = {}, {}, {}
+        b_sb, gap, hid_w, hid_s = {}, {}, {}, {}
 
-        b_sb = {}
+        def pairs_sorted(bank):
+            return bank[:].rearrange("j (p u e) -> j u p e", u=2, e=2)
 
         def product(i, acc, w, s, fmt):
             h, lo = divmod(P * i, HALF)
@@ -112,19 +121,25 @@ def tile_moe_experts_difference_hidden_pl_kernel(
                     rhs=w[:, z, :].bitcast(fmt), rhs_scale=s[:, z, :], start=(z == 0), stop=(z == PASSES - 1),
                 )
 
-        def second(i):
+        def second_expert(i):
             b_ps = psum.tile([P, R], F32, name="b_ps", tag=f"b{i}")
             product(i, b_ps, wb_w, wb_s, FP4X4)
             b_sb[i] = keep.tile([P, 2, P, 2], F32, name=f"b_sb{i}", tag=f"b_sb{i}", align_bytes=64)
-            nc.scalar.copy(out=b_sb[i][:], in_=b_ps[:].rearrange("j (p u e) -> j u p e", u=2, e=2))
+            nc.scalar.copy(out=b_sb[i][:], in_=pairs_sorted(b_ps))
 
-        def first(i):
+        def first_expert(i):
             a_ps = psum.tile([P, R], F32, name="a_ps", tag=f"a{i}")
             product(i, a_ps, wa_w, wa_s, FP8X4)
             gap[i] = ring.tile([P, 2, P, 2], BF16, name="gap", align_bytes=64)
-            nc.vector.tensor_tensor(
-                out=gap[i][:], in0=a_ps[:].rearrange("j (p u e) -> j u p e", u=2, e=2), in1=b_sb[i][:], op=ALU.subtract
+            nc.vector.tensor_tensor(out=gap[i][:], in0=pairs_sorted(a_ps), in1=b_sb[i][:], op=ALU.subtract)
+
+        def deal_columns(name, source, dtype, run, after):
+            dealt = keep.tile([P, PACK, P], dtype, name=name, tag=f"b_sb{after}", align_bytes=64)
+            nc.vector.tensor_copy(
+                out=dealt[:].rearrange("p t (c i) -> p c t i", i=run),
+                in_=source[:].rearrange("p (c i t) -> p c t i", i=run, t=PACK),
             )
+            return dealt
 
         def spread_gate():
             ga_ps = psum.tile([P, TILES, P], F32, name="ga_ps", tag="b0")
@@ -149,17 +164,18 @@ def tile_moe_experts_difference_hidden_pl_kernel(
                 out=hid_w[i][:].bitcast(FP8X4), scales=hid_s[i][:], in_=hid[:].rearrange("p j u e -> p (j u e)")
             )
 
-        def shared(i):
+        def shared_matrix(i):
             tok = slice(P * i, P * (i + 1))
             p_ps = psum.tile([P, PACK, P], F32, name="p_ps", tag=f"a{i}")
             for t in range(PACK):
                 nc.tensor.matmul_mx(
-                    out=p_ps[:, t, :], lhsT=wdp_w[:, t, :].bitcast(FP8X4), lhsT_scale=wdp_s[:, t, :],
+                    out=p_ps[:, t, :], lhsT=wd_dealt_w[:, t, :].bitcast(FP8X4), lhsT_scale=wd_dealt_s[:, t, :],
                     rhs=hid_w[i][:].bitcast(FP8X4), rhs_scale=hid_s[i][:], start=True, stop=True,
                 )
             y = keep.tile([P, PACK, P], F32, name=f"y{i}")
             y16 = ring.tile([P, P, PACK], BF16, name="y16", align_bytes=64)
-            if i == TILES - 1:
+            last = i == TILES - 1
+            if last:
                 nc.vector.tensor_tensor(
                     out=y16[:], in0=p_ps[:].rearrange("p t j -> p j t"),
                     in1=ga_all[:, tok].unsqueeze(2).to_broadcast([P, P, PACK]), op=ALU.mult,
@@ -168,47 +184,45 @@ def tile_moe_experts_difference_hidden_pl_kernel(
                 out=y[:], in0=p_ps[:], in1=ga_all[:, tok].unsqueeze(1).to_broadcast([P, PACK, P]), op=ALU.mult
             )
             nc.sync.dma_start(out=out_rows[:, :, tok], in_=y[:])
-            if i < TILES - 1:
+            if not last:
                 nc.scalar.copy(
-                    out=y16[:].rearrange("p (c i) t -> p c t i", i=4), in_=y[:].rearrange("p t (c i) -> p c t i", i=4)
+                    out=y16[:].rearrange("p (c i) t -> p c t i", i=LINE_WORDS),
+                    in_=y[:].rearrange("p t (c i) -> p c t i", i=LINE_WORDS),
                 )
             nc.vector.quantize_mx(
                 out=y_w[:, tok].bitcast(FP8X4), scales=y_s[:, tok], in_=y16[:].rearrange("p j t -> p (j t)")
             )
             nc.sync.dma_start(out=out_words[:, tok], in_=y_w[:, tok])
 
-        warm = psum.tile([P, R], F32, name="warm", tag="a3")
-        for k in range(WARM):
+        warm = psum.tile([P, R], F32, name="warm", tag=f"a{TILES - 1}")
+        for k in range(WARM_PASSES):
             nc.tensor.matmul_mx(
                 out=warm[:], lhsT=wb_w[:, 0, 0:P].bitcast(FP4X4), lhsT_scale=wb_s[:, 0, 0:P],
                 rhs=wb_w[:, 0, :].bitcast(FP4X4), rhs_scale=wb_s[:, 0, :], start=True, stop=True,
             )
-        second(0)
-        second(1)
-        second(2)
-        first(0)
-        wdp_w = keep.tile([P, PACK, P], I32, name="wdp_w", tag="b_sb0", align_bytes=64)
-        nc.vector.tensor_copy(
-            out=wdp_w[:].rearrange("p t (c i) -> p c t i", i=4), in_=wd_w[:].rearrange("p (c i t) -> p c t i", i=4, t=PACK)
-        )
-        first(1)
-        wdp_s = keep.tile([P, PACK, P], U8, name="wdp_s", tag="b_sb1", align_bytes=64)
-        nc.vector.tensor_copy(
-            out=wdp_s[:].rearrange("p t (c i) -> p c t i", i=16), in_=wd_s[:].rearrange("p (c i t) -> p c t i", i=16, t=PACK)
-        )
+
+        second_expert(0)
+        second_expert(1)
+        first_expert(0)
+        wd_dealt_w = deal_columns("wd_dealt_w", wd_w, I32, LINE_WORDS, after=0)
+        second_expert(2)
+        first_expert(1)
+        wd_dealt_s = deal_columns("wd_dealt_s", wd_s, U8, LINE_BYTES, after=1)
         turn(0)
         spread_gate()
-        second(3)
-        first(2)
+        second_expert(3)
+        first_expert(2)
         turn(1)
-        first(3)
-        shared(0)
+        first_expert(3)
+        shared_matrix(0)
         turn(2)
         turn(3)
-        shared(1)
-        shared(2)
-        shared(3)
+        for i in range(1, TILES):
+            shared_matrix(i)
 
-        for q in range(4):
-            eng = nc.sync if q % 2 == 0 else nc.scalar
-            eng.dma_start(out=out_2[0].bitcast(I32)[4 * q : 4 * q + 4], in_=y_s[32 * q : 32 * q + 4, :].bitcast(I32))
+        for q in range(QUADS):
+            engine = nc.sync if q % 2 == 0 else nc.scalar
+            engine.dma_start(
+                out=out_2[0].bitcast(I32)[LIVE * q : LIVE * (q + 1)],
+                in_=y_s[QUAD * q : QUAD * q + LIVE, :].bitcast(I32),
+            )

@@ -49,7 +49,7 @@ def tile_moe_experts_difference_hidden_pl_kernel(
         wa_s = keep.tile([P, PASSES, R], U8, name="wa_s", align_bytes=64)
         wb_s = keep.tile([P, PASSES, R], U8, name="wb_s", align_bytes=64)
         x_s = keep.tile([P, PASSES, J], U8, name="x_s", align_bytes=64)
-        xs_got = keep.tile([P, J], U8, name="xs_got", tag="gathered_scales", align_bytes=64)
+        xs_got = keep.tile([P, J], U8, name="xs_got", align_bytes=64)
         wd_s = keep.tile([P, N], U8, name="wd_s", align_bytes=64)
         ga_col = keep.tile([P, TILES], F32, name="ga_col")
         ga_all = keep.tile([P, J], F32, name="ga_all")
@@ -81,8 +81,6 @@ def tile_moe_experts_difference_hidden_pl_kernel(
         for z in range(PASSES):
             nc.sync.dma_start(out=xw_win[z][:].bitcast(I32), in_=xt_words[z].bitcast(I32))
         load_planes(nc.sync, wa_s, wa_scales)
-        for r in range(LIVE):
-            nc.sync.dma_start(out=wd_s[r:P:QUAD, :].bitcast(I32), in_=wd_scales[0].bitcast(I32)[r:BLOCKS:LIVE])
 
         nc.vector.tensor_copy(xs_got[:], xs_win[:].indirect(offsets[:]))
         for q in range(QUADS):
@@ -90,19 +88,17 @@ def tile_moe_experts_difference_hidden_pl_kernel(
             nc.scalar.dma_start(
                 out=x_s[QUAD * q : QUAD * q + LIVE].bitcast(I32), in_=xs_got[src : src + PASSES * LIVE, :].bitcast(I32)
             )
-        table_in = keep.tile([P, 1], F32, name="table_in", tag="window", align_bytes=64)
-        nc.vector.memset(table_in[:], 0.0)
-        table_out = keep.tile([P, 1], F32, name="table_out")
-        nc.scalar.activation(out=table_out[:], in_=table_in[:], func=ACT.Relu)
+        wd_w = keep.tile([P, N], I32, name="wd_w", tag="window", align_bytes=64)
+        nc.sync.dma_start(out=wd_w[:], in_=wd_words[0].rearrange("p n t -> p (n t)").bitcast(I32))
+        for r in range(LIVE):
+            nc.sync.dma_start(out=wd_s[r:P:QUAD, :].bitcast(I32), in_=wd_scales[0].bitcast(I32)[r:BLOCKS:LIVE])
+
         x_w = {}
         for h in range(J // HALF):
             for z in range(PASSES):
                 picks = offsets[:, h * HALF // LIST_ROWS : (h + 1) * HALF // LIST_ROWS]
                 x_w[z, h] = keep.tile([P, HALF], U16, name=f"x_w{z}{h}", align_bytes=64)
                 nc.vector.tensor_copy(x_w[z, h][:], xw_win[z][:].indirect(picks))
-
-        wd_w = keep.tile([P, N], I32, name="wd_w", tag="gathered_scales", align_bytes=64)
-        nc.sync.dma_start(out=wd_w[:], in_=wd_words[0].rearrange("p n t -> p (n t)").bitcast(I32))
 
         y_w = keep.tile([P, J], I32, name="y_w", align_bytes=64)
         y_s = keep.tile([P, J], U8, name="y_s", align_bytes=64)
@@ -124,7 +120,7 @@ def tile_moe_experts_difference_hidden_pl_kernel(
         def second_expert(i):
             b_ps = psum.tile([P, R], F32, name="b_ps", tag=f"b{i}")
             product(i, b_ps, wb_w, wb_s, FP4X4)
-            b_sb[i] = keep.tile([P, 2, P, 2], F32, name=f"b_sb{i}", tag=f"b_sb{i}", align_bytes=64)
+            b_sb[i] = keep.tile([P, 2, P, 2], F32, name=f"b_sb{i}", align_bytes=64)
             nc.scalar.copy(out=b_sb[i][:], in_=pairs_sorted(b_ps))
 
         def first_expert(i):
@@ -133,8 +129,8 @@ def tile_moe_experts_difference_hidden_pl_kernel(
             gap[i] = ring.tile([P, 2, P, 2], BF16, name="gap", align_bytes=64)
             nc.vector.tensor_tensor(out=gap[i][:], in0=pairs_sorted(a_ps), in1=b_sb[i][:], op=ALU.subtract)
 
-        def deal_columns(name, source, dtype, run, after):
-            dealt = keep.tile([P, PACK, P], dtype, name=name, tag=f"b_sb{after}", align_bytes=64)
+        def deal_columns(name, source, dtype, run):
+            dealt = keep.tile([P, PACK, P], dtype, name=name, align_bytes=64)
             nc.vector.tensor_copy(
                 out=dealt[:].rearrange("p t (c i) -> p c t i", i=run),
                 in_=source[:].rearrange("p (c i t) -> p c t i", i=run, t=PACK),
@@ -142,10 +138,10 @@ def tile_moe_experts_difference_hidden_pl_kernel(
             return dealt
 
         def spread_gate():
-            ga_ps = psum.tile([P, TILES, P], F32, name="ga_ps", tag="b0")
+            ga_ps = psum.tile([P, TILES, P], F32, name="ga_ps", tag=f"b{TILES - 1}")
             for i in range(TILES):
                 nc.tensor.transpose(ga_ps[:, i, :], ga_col[:, i : i + 1].to_broadcast([P, P]), ident[:])
-            nc.scalar.copy(
+            nc.vector.tensor_copy(
                 out=ga_all[:].rearrange("q (p i) -> q p i", i=TILES), in_=ga_ps[:].rearrange("q i p -> q p i")
             )
 
@@ -201,15 +197,16 @@ def tile_moe_experts_difference_hidden_pl_kernel(
                 rhs=wb_w[:, 0, :].bitcast(FP4X4), rhs_scale=wb_s[:, 0, :], start=True, stop=True,
             )
 
+        spread_gate()
+        wd_dealt_w = deal_columns("wd_dealt_w", wd_w, I32, LINE_WORDS)
+        wd_dealt_s = deal_columns("wd_dealt_s", wd_s, U8, LINE_BYTES)
+
         second_expert(0)
         second_expert(1)
         first_expert(0)
-        wd_dealt_w = deal_columns("wd_dealt_w", wd_w, I32, LINE_WORDS, after=0)
         second_expert(2)
         first_expert(1)
-        wd_dealt_s = deal_columns("wd_dealt_s", wd_s, U8, LINE_BYTES, after=1)
         turn(0)
-        spread_gate()
         second_expert(3)
         first_expert(2)
         turn(1)

from contextlib import ExitStack

import concourse.mybir as mybir
from concourse.masks import make_identity

K, T, J, N, R = 1024, 2048, 512, 512, 512
FLOPS = 2 * (2 * K * R * J + R * N * J)

F32 = mybir.dt.float32
BF16 = mybir.dt.bfloat16
I32 = mybir.dt.int32
U16 = mybir.dt.uint16
U8 = mybir.dt.uint8
FP8X4 = mybir.dt.float8_e4m3fn_x4
FP4X4 = mybir.dt.float4_e2m1fn_x4
ALU = mybir.AluOpType
ACT = mybir.ActivationFunctionType

P = 128
PACK = 4
PASSES = K // (P * PACK)
QUAD = 32
QUADS = P // QUAD
LIVE = 4
BLOCKS = QUADS * LIVE
TILES = J // P
HALF = J // 2
LIST_ROWS = 16
SCALE_ROW0 = P - PASSES * BLOCKS
LINE_WORDS, LINE_BYTES = 4, 16
WARM_PASSES = 4


def tile_moe_experts_difference_hidden_pl_kernel(
    tc, xt_words, xt_scales, wa_words, wa_scales, wb_words, wb_scales, wd_words, wd_scales, ga, offs,
    out_0, out_1, out_2,
):
    nc = tc.nc
    with ExitStack() as ctx:
        keep = ctx.enter_context(tc.tile_pool(name="keep", bufs=1))
        ring = ctx.enter_context(tc.tile_pool(name="ring", bufs=TILES))
        psum = ctx.enter_context(tc.psum_pool(name="psum", bufs=1))

        offsets = keep.tile([P, J // LIST_ROWS], U16, name="offsets")
        xs_win = keep.tile([P, T], U8, name="xs_win", tag="window", align_bytes=64)
        xw_win = [keep.tile([P, T], U16, name=f"xw_win{z}", align_bytes=64) for z in range(PASSES)]
        wa_w = keep.tile([P, PASSES, R], I32, name="wa_w", align_bytes=64)
        wb_w = keep.tile([P, PASSES, R], U16, name="wb_w", align_bytes=64)
        wa_s = keep.tile([P, PASSES, R], U8, name="wa_s", align_bytes=64)
        wb_s = keep.tile([P, PASSES, R], U8, name="wb_s", align_bytes=64)
        x_s = keep.tile([P, PASSES, J], U8, name="x_s", align_bytes=64)
        xs_got = keep.tile([P, J], U8, name="xs_got", align_bytes=64)
        wd_s = keep.tile([P, N], U8, name="wd_s", align_bytes=64)
        ga_col = keep.tile([P, TILES], F32, name="ga_col")
        ga_all = keep.tile([P, J], F32, name="ga_all")
        ident = keep.tile([P, P], F32, name="ident")

        def flat_i32(planes):
            return planes[:].rearrange("p z n -> p (z n)").bitcast(I32)

        def load_planes(engine, planes, rows):
            by_row = rows.rearrange("z q n -> q z n").bitcast(I32)
            for r in range(LIVE):
                engine.dma_start(out=planes[r:P:QUAD].bitcast(I32), in_=by_row[r:BLOCKS:LIVE])

        nc.sync.dma_start(offsets[:], offs)
        nc.scalar.dma_start(
            out=xs_win[SCALE_ROW0:P, :].bitcast(I32), in_=xt_scales.rearrange("z q n -> q z n").bitcast(I32)
        )
        nc.vector.memset(flat_i32(wb_s), 0)
        nc.vector.memset(xs_win[0:SCALE_ROW0, :].bitcast(I32), 0)
        nc.vector.memset(flat_i32(wa_s), 0)
        nc.vector.memset(flat_i32(x_s), 0)
        make_identity(nc, ident[:])
        nc.gpsimd.memset(wd_s[:].bitcast(I32), 0)
        nc.gpsimd.dma_start(out=wa_w[:], in_=wa_words.rearrange("z p n t -> p z (n t)").bitcast(I32))
        nc.gpsimd.dma_start(out=ga_col[:], in_=ga.rearrange("o (p i) -> (o p) i", i=TILES))

        load_planes(nc.scalar, wb_s, wb_scales)
        nc.sync.dma_start(out=wb_w[:].bitcast(I32), in_=wb_words.rearrange("z p n -> p z n").bitcast(I32))
        for z in range(PASSES):
            nc.sync.dma_start(out=xw_win[z][:].bitcast(I32), in_=xt_words[z].bitcast(I32))
        load_planes(nc.sync, wa_s, wa_scales)

        nc.vector.tensor_copy(xs_got[:], xs_win[:].indirect(offsets[:]))
        for q in range(QUADS):
            src = SCALE_ROW0 + PASSES * LIVE * q
            nc.scalar.dma_start(
                out=x_s[QUAD * q : QUAD * q + LIVE].bitcast(I32), in_=xs_got[src : src + PASSES * LIVE, :].bitcast(I32)
            )
        wd_w = keep.tile([P, N], I32, name="wd_w", tag="window", align_bytes=64)
        nc.sync.dma_start(out=wd_w[:], in_=wd_words[0].rearrange("p n t -> p (n t)").bitcast(I32))
        for r in range(LIVE):
            nc.sync.dma_start(out=wd_s[r:P:QUAD, :].bitcast(I32), in_=wd_scales[0].bitcast(I32)[r:BLOCKS:LIVE])

        x_w = {}
        for h in range(J // HALF):
            for z in range(PASSES):
                picks = offsets[:, h * HALF // LIST_ROWS : (h + 1) * HALF // LIST_ROWS]
                x_w[z, h] = keep.tile([P, HALF], U16, name=f"x_w{z}{h}", align_bytes=64)
                nc.vector.tensor_copy(x_w[z, h][:], xw_win[z][:].indirect(picks))

        y_w = keep.tile([P, J], I32, name="y_w", align_bytes=64)
        y_s = keep.tile([P, J], U8, name="y_s", align_bytes=64)
        out_rows = out_0.rearrange("(p t) j -> p t j", t=PACK)
        out_words = out_1[0].rearrange("p c t -> p (c t)").bitcast(I32)
        b_sb, gap, hid_w, hid_s = {}, {}, {}, {}

        def pairs_sorted(bank):
            return bank[:].rearrange("j (p u e) -> j u p e", u=2, e=2)

        def product(i, acc, w, s, fmt):
            h, lo = divmod(P * i, HALF)
            for z in range(PASSES):
                nc.tensor.matmul_mx(
                    out=acc[:], lhsT=x_w[z, h][:, lo : lo + P].bitcast(FP4X4), lhsT_scale=x_s[:, z, P * i : P * (i + 1)],
                    rhs=w[:, z, :].bitcast(fmt), rhs_scale=s[:, z, :], start=(z == 0), stop=(z == PASSES - 1),
                )

        def second_expert(i):
            b_ps = psum.tile([P, R], F32, name="b_ps", tag=f"b{i}")
            product(i, b_ps, wb_w, wb_s, FP4X4)
            b_sb[i] = keep.tile([P, 2, P, 2], F32, name=f"b_sb{i}", align_bytes=64)
            nc.scalar.copy(out=b_sb[i][:], in_=pairs_sorted(b_ps))

        def first_expert(i):
            a_ps = psum.tile([P, R], F32, name="a_ps", tag=f"a{i}")
            product(i, a_ps, wa_w, wa_s, FP8X4)
            gap[i] = ring.tile([P, 2, P, 2], BF16, name="gap", align_bytes=64)
            nc.vector.tensor_tensor(out=gap[i][:], in0=pairs_sorted(a_ps), in1=b_sb[i][:], op=ALU.subtract)

        def deal_columns(name, source, dtype, run):
            dealt = keep.tile([P, PACK, P], dtype, name=name, align_bytes=64)
            nc.vector.tensor_copy(
                out=dealt[:].rearrange("p t (c i) -> p c t i", i=run),
                in_=source[:].rearrange("p (c i t) -> p c t i", i=run, t=PACK),
            )
            return dealt

        def spread_gate():
            ga_ps = psum.tile([P, TILES, P], F32, name="ga_ps", tag=f"b{TILES - 1}")
            for i in range(TILES):
                nc.tensor.transpose(ga_ps[:, i, :], ga_col[:, i : i + 1].to_broadcast([P, P]), ident[:])
            nc.vector.tensor_copy(
                out=ga_all[:].rearrange("q (p i) -> q p i", i=TILES), in_=ga_ps[:].rearrange("q i p -> q p i")
            )

        def turn(i):
            pairs = gap[i][:].rearrange("j u p e -> j (u p e)").bitcast(F32)
            tr_ps = psum.tile([P, 2 * P], F32, name="tr_ps", tag=f"a{i}")
            for u in range(2):
                nc.tensor.transpose(tr_ps[:, P * u : P * (u + 1)], pairs[:, P * u : P * (u + 1)], ident[:])
            hid = ring.tile([P, P, 2, 2], BF16, name="hid", align_bytes=64)
            nc.scalar.activation(
                out=hid[:], in_=tr_ps[:].bitcast(BF16).rearrange("p (u j e) -> p j u e", u=2, e=2), func=ACT.Relu
            )
            hid_w[i] = ring.tile([P, P], I32, name="hid_w", align_bytes=64)
            hid_s[i] = ring.tile([P, P], U8, name="hid_s", align_bytes=64)
            nc.vector.quantize_mx(
                out=hid_w[i][:].bitcast(FP8X4), scales=hid_s[i][:], in_=hid[:].rearrange("p j u e -> p (j u e)")
            )

        def shared_matrix(i):
            tok = slice(P * i, P * (i + 1))
            p_ps = psum.tile([P, PACK, P], F32, name="p_ps", tag=f"a{i}")
            for t in range(PACK):
                nc.tensor.matmul_mx(
                    out=p_ps[:, t, :], lhsT=wd_dealt_w[:, t, :].bitcast(FP8X4), lhsT_scale=wd_dealt_s[:, t, :],
                    rhs=hid_w[i][:].bitcast(FP8X4), rhs_scale=hid_s[i][:], start=True, stop=True,
                )
            y = keep.tile([P, PACK, P], F32, name=f"y{i}")
            y16 = ring.tile([P, P, PACK], BF16, name="y16", align_bytes=64)
            last = i == TILES - 1
            if last:
                nc.vector.tensor_tensor(
                    out=y16[:], in0=p_ps[:].rearrange("p t j -> p j t"),
                    in1=ga_all[:, tok].unsqueeze(2).to_broadcast([P, P, PACK]), op=ALU.mult,
                )
            nc.vector.tensor_tensor(
                out=y[:], in0=p_ps[:], in1=ga_all[:, tok].unsqueeze(1).to_broadcast([P, PACK, P]), op=ALU.mult
            )
            nc.sync.dma_start(out=out_rows[:, :, tok], in_=y[:])
            if not last:
                nc.scalar.copy(
                    out=y16[:].rearrange("p (c i) t -> p c t i", i=LINE_WORDS),
                    in_=y[:].rearrange("p t (c i) -> p c t i", i=LINE_WORDS),
                )
            nc.vector.quantize_mx(
                out=y_w[:, tok].bitcast(FP8X4), scales=y_s[:, tok], in_=y16[:].rearrange("p j t -> p (j t)")
            )
            nc.sync.dma_start(out=out_words[:, tok], in_=y_w[:, tok])

        warm = psum.tile([P, R], F32, name="warm", tag=f"a{TILES - 1}")
        for k in range(WARM_PASSES):
            nc.tensor.matmul_mx(
                out=warm[:], lhsT=wb_w[:, 0, 0:P].bitcast(FP4X4), lhsT_scale=wb_s[:, 0, 0:P],
                rhs=wb_w[:, 0, :].bitcast(FP4X4), rhs_scale=wb_s[:, 0, :], start=True, stop=True,
            )

        spread_gate()
        wd_dealt_w = deal_columns("wd_dealt_w", wd_w, I32, LINE_WORDS)
        wd_dealt_s = deal_columns("wd_dealt_s", wd_s, U8, LINE_BYTES)

        second_expert(0)
        second_expert(1)
        first_expert(0)
        second_expert(2)
        first_expert(1)
        turn(0)
        second_expert(3)
        first_expert(2)
        turn(1)
        first_expert(3)
        shared_matrix(0)
        turn(2)
        turn(3)
        for i in range(1, TILES):
            shared_matrix(i)

        for q in range(QUADS):
            engine = nc.sync if q % 2 == 0 else nc.scalar
            engine.dma_start(
                out=out_2[0].bitcast(I32)[LIVE * q : LIVE * (q + 1)],
                in_=y_s[QUAD * q : QUAD * q + LIVE, :].bitcast(I32),
            )
